import numpy as np
import ml_dtypes


def mxq(x, axis, fmt="e4m3"):
    dtype, down = {"e4m3": (ml_dtypes.float8_e4m3fn, 7), "e5m2": (ml_dtypes.float8_e5m2, 14)}[fmt]
    v = np.moveaxis(np.asarray(x, np.float32).astype(ml_dtypes.bfloat16).astype(np.float64), axis, -1)
    blocks = v.reshape(v.shape[:-1] + (-1, 32))
    amax = np.abs(blocks).max(-1, keepdims=True)
    byte = np.maximum(np.where(amax > 0, np.frexp(amax)[1] - 1 + 127, 0) - down, 1)
    scale = np.exp2(byte - 127.0)
    codes = (blocks / scale).astype(np.float32).astype(dtype).astype(np.float64)
    return np.moveaxis((codes * scale).reshape(v.shape), -1, axis)


WIDE = False


def mx_kscale(k):
    if not WIDE:
        return np.ones(k)
    levels = np.array([10, -10, 5, -5, 0])
    if k % 512:
        return np.exp2(np.random.permutation(np.resize(levels, k // 32))).repeat(32)
    a = np.empty((k // 512, 16))
    for p in range(k // 512):
        a[p, :8] = np.random.permutation(np.resize(levels, 8))
        for g in range(8):
            far = levels[np.abs(levels - a[p, g]) >= 10]
            a[p, g + 8] = far[np.random.randint(len(far))]
    return np.exp2(a.ravel()).repeat(32)


def f64(x):
    return np.asarray(x).astype(np.float64)


def striped8(idx):
    return np.asarray(idx).reshape(8, -1, 16).transpose(0, 2, 1).reshape(128, -1).astype(np.uint16)


def unstriped8(offs):
    return offs.reshape(8, 16, -1).transpose(0, 2, 1).reshape(8, -1).astype(np.int64)


def pick8(x, idx, run):
    r = np.arange(len(x))
    return x[r[:, None], idx[r % (8 * run) // run]]


E2M1 = np.array([0.0, 0.5, 1.0, 1.5, 2.0, 3.0, 4.0, 6.0, -0.0, -0.5, -1.0, -1.5, -2.0, -3.0, -4.0, -6.0])


def pack_weight(w, fmt):
    k, n = w.shape
    w = f64(np.asarray(w, np.float32).astype(ml_dtypes.bfloat16)).reshape(k // 32, 32, n)
    amax = np.abs(w).max(1)
    if fmt == "e4m3":
        byte = np.frexp(amax)[1] - 1 + 127 - 7
    else:
        mant, ex = np.frexp(amax / 6.0)
        byte = np.where(mant > 0.5, ex, ex - 1) + 127
    byte = np.clip(np.where(amax > 0, byte, 1), 1, 254)
    scaled = (w * np.exp2(127.0 - byte)[:, None, :]).reshape(k, n).astype(np.float32)
    by_word = np.ascontiguousarray(scaled.reshape(k // 512, 128, 4, n).transpose(0, 1, 3, 2))
    if fmt == "e4m3":
        words = by_word.astype(ml_dtypes.float8_e4m3fn).view(np.uint8)
    else:
        c = by_word.astype(ml_dtypes.float4_e2m1fn).view(np.uint8) & 0xF
        words = (c[..., 0::2] | (c[..., 1::2] << 4)).reshape(k // 512, 128, 2 * n)
    return np.ascontiguousarray(words), np.ascontiguousarray(byte.astype(np.uint8).reshape(k // 512, 16, n))


def unpack_weight(words, scales, fmt):
    g, _, n = scales.shape
    words = np.ascontiguousarray(words).reshape(g, 128, n, -1)
    if fmt == "e4m3":
        vals = words.view(ml_dtypes.float8_e4m3fn).astype(np.float64)
    else:
        nib = np.empty((g, 128, n, 4), np.uint8)
        nib[..., 0::2] = words & 0xF
        nib[..., 1::2] = words >> 4
        vals = E2M1[nib]
    vals = vals * np.repeat(np.exp2(scales.astype(np.float64) - 127.0), 8, axis=1)[..., None]
    return vals.transpose(0, 1, 3, 2).reshape(g * 512, n)


def bf(x):
    return np.asarray(x, np.float32).astype(ml_dtypes.bfloat16)


def planes(Y):
    r, m = Y.shape
    b = f64(bf(Y)).reshape(r // 32, 32, m)
    amax = np.abs(b).max(1)
    byte = np.clip(np.where(amax > 0, np.frexp(amax)[1] - 1 + 127 - 7, 1), 1, 254)
    codes = (b * np.exp2(127.0 - byte)[:, None, :]).reshape(r, m).astype(np.float32).astype(ml_dtypes.float8_e4m3fn).view(np.uint8)
    words = codes.reshape(r // 512, 128, 4, m).transpose(0, 1, 3, 2)
    return np.ascontiguousarray(words), np.ascontiguousarray(byte.astype(np.uint8).reshape(r // 512, 16, m))


K, T, J, N, L = 512, 512, 512, 512, 512


def setup_inputs():
    n = np.random.standard_normal
    idx = np.stack([np.random.randint(0, T, J) for _ in range(8)])
    fk = mx_kscale(K)
    fl = mx_kscale(L)
    xtp = pack_weight(n((K, T)) / fk[:, None], "e2m1")
    xip = pack_weight(n((L, J)) / fl[:, None], "e4m3")
    wip = pack_weight(n((L, N)) * 1 / np.sqrt(L) * fl[:, None], "e2m1")
    return {
        "xt_words": xtp[0],
        "xt_scales": xtp[1],
        "w": (n((K, N)) * 1 / np.sqrt(K) * fk[:, None]).astype(np.float32),
        "xi_words": xip[0],
        "xi_scales": xip[1],
        "wi_words": wip[0],
        "wi_scales": wip[1],
        "offs": striped8(idx),
    }


def reference(xt_words, xt_scales, w, xi_words, xi_scales, wi_words, wi_scales, offs):
    idx = unstriped8(offs)
    xtu = unpack_weight(xt_words, xt_scales, "e2m1")
    xiu = unpack_weight(xi_words, xi_scales, "e4m3")
    wiu = unpack_weight(wi_words, wi_scales, "e2m1")
    wq = mxq(f64(w), 0, "e4m3")
    z = wq.T @ xtu
    u = pick8(z, idx, 64)
    q = wiu.T @ xiu
    y = u * 1.0 / (np.max(np.abs(u), axis=1, keepdims=True) + 0.5) + 0.3 * q
    words, scales = planes(y)
    return y, words, scales

@@ -1,0 +1,196 @@
+from contextlib import ExitStack
+
+import concourse.mybir as mybir
+
+F32 = mybir.dt.float32
+BF16 = mybir.dt.bfloat16
+I32 = mybir.dt.int32
+U32 = mybir.dt.uint32
+U16 = mybir.dt.uint16
+U8 = mybir.dt.uint8
+FP8X4 = mybir.dt.float8_e4m3fn_x4
+FP4X4 = mybir.dt.float4_e2m1fn_x4
+ALU = mybir.AluOpType
+ACT = mybir.ActivationFunctionType
+AXIS = mybir.AxisListType
+
+P = 128
+PACK = 4
+D = 512
+HALF = D // 2
+FLOPS = 2 * 2 * D * D * D
+CAST_SPLIT = 44
+
+
+def tile_list_head_scaled_by_peak_pl_kernel(tc, xt_words, xt_scales, w, xi_words, xi_scales, wi_words, wi_scales, offs, out_0, out_1, out_2):
+    nc = tc.nc
+    with ExitStack() as ctx:
+        keep = ctx.enter_context(tc.tile_pool(name="keep", bufs=1))
+        ring = ctx.enter_context(tc.tile_pool(name="ring", bufs=3))
+        psum = ctx.enter_context(tc.psum_pool(name="psum", bufs=1))
+
+        def load_scales(queue, plane, rows):
+            for quad in range(4):
+                queue.dma_start(out=plane[32 * quad : 32 * quad + 4, :].bitcast(I32), in_=rows[0, 4 * quad : 4 * quad + 4, :].bitcast(I32))
+
+        xt_plane = keep.tile([P, D], U8, name="xt_plane", align_bytes=64)
+        xi_plane = keep.tile([P, D], U8, name="xi_plane", align_bytes=64)
+        wi_plane_raw = keep.tile([P, D], U8, name="wi_plane_raw", align_bytes=64)
+        nc.gpsimd.memset(xt_plane[:].bitcast(I32), 0)
+        nc.gpsimd.memset(wi_plane_raw[:].bitcast(I32), 0)
+        nc.vector.memset(xi_plane[:].bitcast(I32), 0)
+
+        load_scales(nc.gpsimd, wi_plane_raw, wi_scales)
+        w_rows = w.rearrange("(p j) c -> p j c", j=PACK)
+        w_raw = []
+        for h in range(2):
+            raw = keep.tile([P, PACK, HALF], F32, name="w_raw%d" % h)
+            nc.sync.dma_start(out=raw[:], in_=w_rows[:, :, h * HALF : (h + 1) * HALF])
+            w_raw.append(raw)
+        xt_codes = keep.tile([P, 2 * D], U8, name="xt_codes", align_bytes=64)
+        nc.sync.dma_start(out=xt_codes[:].bitcast(I32), in_=xt_words[0].bitcast(I32))
+        load_scales(nc.sync, xt_plane, xt_scales)
+        wi_raw = keep.tile([P, 2 * D], U8, name="wi_raw", align_bytes=64)
+        nc.sync.dma_start(out=wi_raw[:].bitcast(I32), in_=wi_words[0].bitcast(I32))
+        offsets = keep.tile([P, D // 16], U16, name="offsets")
+        nc.sync.dma_start(offsets[:], offs)
+        xi_codes = keep.tile([P, PACK * D], U8, name="xi_codes", align_bytes=64)
+        nc.sync.dma_start(out=xi_codes[:].bitcast(I32), in_=xi_words[0].rearrange("p c r -> p (c r)").bitcast(I32))
+        load_scales(nc.sync, xi_plane, xi_scales)
+
+        w_bf = keep.tile([P, PACK, P, PACK], BF16, name="w_bf", tag="staging", align_bytes=64)
+
+        def cast_views(h, m0, m1):
+            dst = w_bf[:, :, 64 * h + m0 : 64 * h + m1, :].rearrange("p t m j -> p m t j")
+            src = w_raw[h][:, :, PACK * m0 : PACK * m1].rearrange("p j (m t) -> p m t j", t=PACK)
+            return dst, src
+
+        dst, src = cast_views(0, 0, 64)
+        nc.vector.tensor_copy(out=dst, in_=src)
+        dst, src = cast_views(1, 0, CAST_SPLIT)
+        nc.vector.tensor_copy(out=dst, in_=src)
+        dst, src = cast_views(1, CAST_SPLIT, 64)
+        nc.scalar.activation(out=dst, in_=src, func=ACT.Copy)
+
+        z_bank = []
+        for t in range(PACK):
+            codes = keep.tile([P, P], U32, name="w_codes%d" % t, align_bytes=64)
+            plane = keep.tile([P, P], U8, name="w_plane%d" % t, align_bytes=64)
+            nc.vector.quantize_mx(out=codes[:].bitcast(FP8X4), scales=plane[:], in_=w_bf[:, t, :, :].rearrange("p m j -> p (m j)"))
+            bank = psum.tile([P, D], F32, name="z_bank%d" % t)
+            nc.tensor.matmul_mx(out=bank[:], lhsT=codes[:].bitcast(FP8X4), lhsT_scale=plane[:], rhs=xt_codes[:].bitcast(FP4X4), rhs_scale=xt_plane[:], start=True, stop=True)
+            z_bank.append(bank)
+
+        wi_codes = keep.tile([P, 2 * D], U8, name="wi_codes", align_bytes=64)
+        wi_plane = keep.tile([P, D], U8, name="wi_plane", tag="staging", align_bytes=64)
+        nc.scalar.copy(out=wi_codes[:].bitcast(U16).rearrange("p (t m) -> p t m", t=PACK), in_=wi_raw[:].bitcast(U16).rearrange("p (m t) -> p t m", t=PACK))
+        nc.gpsimd.tensor_copy(out=wi_plane[:].rearrange("p (t m) -> p t m", t=PACK), in_=wi_plane_raw[:].rearrange("p (m t) -> p t m", t=PACK))
+        q_bank = []
+        for t in range(PACK):
+            bank = psum.tile([P, D], F32, name="q_bank%d" % t)
+            nc.tensor.matmul_mx(out=bank[:], lhsT=wi_codes[:, 2 * P * t : 2 * P * (t + 1)].bitcast(FP4X4), lhsT_scale=wi_plane[:, P * t : P * (t + 1)], rhs=xi_codes[:].bitcast(FP8X4), rhs_scale=xi_plane[:], start=True, stop=True)
+            q_bank.append(bank)
+
+        z = [keep.tile([P, D], F32, name="z%d" % t) for t in range(PACK)]
+        u = [keep.tile([P, D], F32, name="u%d" % t) for t in range(PACK)]
+        y = keep.tile([P, PACK, D], F32, name="y")
+        y_rows = out_0.rearrange("(p t) j -> p t j", t=PACK)
+        work = {}
+
+        def leave(t, on_vector):
+            if on_vector:
+                nc.vector.tensor_copy(out=z[t][:], in_=z_bank[t][:])
+            else:
+                nc.scalar.copy(out=z[t][:], in_=z_bank[t][:])
+
+        def look_up(t, h, on_vector):
+            picked = z[t][:].indirect(offsets[:, 16 * h : 16 * (h + 1)])
+            if on_vector:
+                nc.vector.tensor_copy(out=u[t][:, h * HALF : (h + 1) * HALF], in_=picked)
+            else:
+                nc.scalar.activation(out=u[t][:, h * HALF : (h + 1) * HALF], in_=picked, func=ACT.Copy)
+
+        def find_peak(t):
+            work[t] = ring.tile([P, 8 + D], F32, name="work")
+            nc.vector.tensor_reduce(out=work[t][:, 0:1], in_=u[t][:], axis=AXIS.X, op=ALU.max, apply_absolute_value=True)
+
+        def add_half(t):
+            nc.vector.tensor_scalar(out=work[t][:, 1:2], in0=work[t][:, 0:1], scalar1=0.5, scalar2=None, op0=ALU.add)
+
+        def invert(t):
+            nc.vector.reciprocal(out=work[t][:, 2:3], in_=work[t][:, 1:2])
+
+        def normalise(t):
+            nc.gpsimd.tensor_scalar(out=work[t][:, 8:], in0=u[t][:], scalar1=work[t][:, 2:3], scalar2=0.0, op0=ALU.mult, op1=ALU.add)
+
+        def scale_q(t):
+            nc.scalar.activation(out=work[t][:, 8:], in_=q_bank[t][:], func=ACT.Copy, scale=0.3)
+
+        def combine_from_bank(t):
+            nc.vector.scalar_tensor_tensor(out=y[:, t, :], in0=q_bank[t][:], scalar=0.3, in1=work[t][:, 8:], op0=ALU.mult, op1=ALU.add)
+
+        def combine(t, c0, c1):
+            nc.vector.scalar_tensor_tensor(out=y[:, t, c0:c1], in0=u[t][:, c0:c1], scalar=work[t][:, 2:3], in1=work[t][:, 8 + c0 : 8 + c1], op0=ALU.mult, op1=ALU.add)
+
+        def store(t):
+            nc.sync.dma_start(out=y_rows[:, t, :], in_=y[:, t, :])
+
+        leave(0, False)
+        leave(1, True)
+        look_up(0, 0, False)
+        look_up(0, 1, False)
+        look_up(1, 0, True)
+        look_up(1, 1, False)
+        find_peak(0)
+        leave(2, False)
+        find_peak(1)
+        add_half(0)
+        add_half(1)
+        invert(0)
+        invert(1)
+        normalise(0)
+        normalise(1)
+        look_up(2, 0, False)
+        look_up(2, 1, False)
+        leave(3, True)
+        look_up(3, 0, False)
+        look_up(3, 1, False)
+        find_peak(2)
+        scale_q(2)
+        combine_from_bank(0)
+        store(0)
+        add_half(2)
+        combine_from_bank(1)
+        store(1)
+        invert(2)
+        find_peak(3)
+        scale_q(3)
+        add_half(3)
+        combine(2, 0, D)
+        store(2)
+        invert(3)
+        combine(3, 0, HALF)
+        combine(3, HALF, D)
+        store(3)
+
+        y_codes = keep.tile([P, D], U32, name="y_codes", align_bytes=64)
+        y_plane = keep.tile([P, D], U8, name="y_plane", align_bytes=64)
+        y_bf = [keep.tile([P, HALF, PACK], BF16, name="y_bf%d" % h, align_bytes=64) for h in range(2)]
+
+        def weave_views(h):
+            dst = y_bf[h][:].rearrange("p (c i) t -> p c t i", i=4)
+            src = y[:, :, h * HALF : (h + 1) * HALF].rearrange("p t (c i) -> p c t i", i=4)
+            return dst, src
+
+        dst, src = weave_views(0)
+        nc.scalar.activation(out=dst, in_=src, func=ACT.Copy)
+        dst, src = weave_views(1)
+        nc.vector.tensor_copy(out=dst, in_=src)
+        code_rows = out_1[0].rearrange("p c r -> p (c r)").bitcast(I32)
+        for h in (1, 0):
+            cols = slice(h * HALF, (h + 1) * HALF)
+            nc.vector.quantize_mx(out=y_codes[:, cols].bitcast(FP8X4), scales=y_plane[:, cols], in_=y_bf[h][:].rearrange("p c t -> p (c t)"))
+            nc.sync.dma_start(out=code_rows[:, cols], in_=y_codes[:, cols].bitcast(I32))
+        for quad in range(4):
+            queue = nc.sync if quad == 3 else nc.scalar
+            queue.dma_start(out=out_2[0, 4 * quad : 4 * quad + 4, :].bitcast(I32), in_=y_plane[32 * quad : 32 * quad + 4, :].bitcast(I32))

@@ -19,14 +19,15 @@ PACK = 4
 D = 512
 HALF = D // 2
 FLOPS = 2 * 2 * D * D * D
-CAST_SPLIT = 44
+W_CHUNKS = ((0, 52, 80), (80, 112, 128))
+WEAVE_SPLIT = 192
 
 
 def tile_list_head_scaled_by_peak_pl_kernel(tc, xt_words, xt_scales, w, xi_words, xi_scales, wi_words, wi_scales, offs, out_0, out_1, out_2):
     nc = tc.nc
     with ExitStack() as ctx:
         keep = ctx.enter_context(tc.tile_pool(name="keep", bufs=1))
-        ring = ctx.enter_context(tc.tile_pool(name="ring", bufs=3))
+        ring = ctx.enter_context(tc.tile_pool(name="ring", bufs=2))
         psum = ctx.enter_context(tc.psum_pool(name="psum", bufs=1))
 
         def load_scales(queue, plane, rows):
@@ -43,9 +44,9 @@ def tile_list_head_scaled_by_peak_pl_kernel(tc, xt_words, xt_scales, w, xi_words
         load_scales(nc.gpsimd, wi_plane_raw, wi_scales)
         w_rows = w.rearrange("(p j) c -> p j c", j=PACK)
         w_raw = []
-        for h in range(2):
-            raw = keep.tile([P, PACK, HALF], F32, name="w_raw%d" % h)
-            nc.sync.dma_start(out=raw[:], in_=w_rows[:, :, h * HALF : (h + 1) * HALF])
+        for h, (m0, m1, m2) in enumerate(W_CHUNKS):
+            raw = keep.tile([P, PACK, PACK * (m2 - m0)], F32, name="w_raw%d" % h)
+            nc.sync.dma_start(out=raw[:], in_=w_rows[:, :, PACK * m0 : PACK * m2])
             w_raw.append(raw)
         xt_codes = keep.tile([P, 2 * D], U8, name="xt_codes", align_bytes=64)
         nc.sync.dma_start(out=xt_codes[:].bitcast(I32), in_=xt_words[0].bitcast(I32))
@@ -61,25 +62,27 @@ def tile_list_head_scaled_by_peak_pl_kernel(tc, xt_words, xt_scales, w, xi_words
         w_bf = keep.tile([P, PACK, P, PACK], BF16, name="w_bf", tag="staging", align_bytes=64)
 
         def cast_views(h, m0, m1):
-            dst = w_bf[:, :, 64 * h + m0 : 64 * h + m1, :].rearrange("p t m j -> p m t j")
-            src = w_raw[h][:, :, PACK * m0 : PACK * m1].rearrange("p j (m t) -> p m t j", t=PACK)
+            first = W_CHUNKS[h][0]
+            dst = w_bf[:, :, m0:m1, :].rearrange("p t m j -> p m t j")
+            src = w_raw[h][:, :, PACK * (m0 - first) : PACK * (m1 - first)].rearrange("p j (m t) -> p m t j", t=PACK)
             return dst, src
 
-        dst, src = cast_views(0, 0, 64)
-        nc.vector.tensor_copy(out=dst, in_=src)
-        dst, src = cast_views(1, 0, CAST_SPLIT)
-        nc.vector.tensor_copy(out=dst, in_=src)
-        dst, src = cast_views(1, CAST_SPLIT, 64)
-        nc.scalar.activation(out=dst, in_=src, func=ACT.Copy)
+        for h, (m0, m1, m2) in enumerate(W_CHUNKS):
+            dst, src = cast_views(h, m0, m1)
+            nc.vector.tensor_copy(out=dst, in_=src)
+            dst, src = cast_views(h, m1, m2)
+            nc.scalar.activation(out=dst, in_=src, func=ACT.Copy)
 
         z_bank = []
         for t in range(PACK):
             codes = keep.tile([P, P], U32, name="w_codes%d" % t, align_bytes=64)
             plane = keep.tile([P, P], U8, name="w_plane%d" % t, align_bytes=64)
             nc.vector.quantize_mx(out=codes[:].bitcast(FP8X4), scales=plane[:], in_=w_bf[:, t, :, :].rearrange("p m j -> p (m j)"))
-            bank = psum.tile([P, D], F32, name="z_bank%d" % t)
-            nc.tensor.matmul_mx(out=bank[:], lhsT=codes[:].bitcast(FP8X4), lhsT_scale=plane[:], rhs=xt_codes[:].bitcast(FP4X4), rhs_scale=xt_plane[:], start=True, stop=True)
-            z_bank.append(bank)
+            width = HALF if t == 0 else D
+            for c0 in range(0, D, width):
+                bank = psum.tile([P, width], F32, name="z_bank%d" % len(z_bank))
+                nc.tensor.matmul_mx(out=bank[:], lhsT=codes[:].bitcast(FP8X4), lhsT_scale=plane[:], rhs=xt_codes[:, 2 * c0 : 2 * (c0 + width)].bitcast(FP4X4), rhs_scale=xt_plane[:, c0 : c0 + width], start=True, stop=True)
+                z_bank.append(bank)
 
         wi_codes = keep.tile([P, 2 * D], U8, name="wi_codes", align_bytes=64)
         wi_plane = keep.tile([P, D], U8, name="wi_plane", tag="staging", align_bytes=64)
@@ -87,21 +90,23 @@ def tile_list_head_scaled_by_peak_pl_kernel(tc, xt_words, xt_scales, w, xi_words
         nc.gpsimd.tensor_copy(out=wi_plane[:].rearrange("p (t m) -> p t m", t=PACK), in_=wi_plane_raw[:].rearrange("p (m t) -> p t m", t=PACK))
         q_bank = []
         for t in range(PACK):
-            bank = psum.tile([P, D], F32, name="q_bank%d" % t)
+            bank = psum.tile([P, D], F32, name="q_bank%d" % t, tag="z_bank0" if t == 3 else "q_bank%d" % t)
             nc.tensor.matmul_mx(out=bank[:], lhsT=wi_codes[:, 2 * P * t : 2 * P * (t + 1)].bitcast(FP4X4), lhsT_scale=wi_plane[:, P * t : P * (t + 1)], rhs=xi_codes[:].bitcast(FP8X4), rhs_scale=xi_plane[:], start=True, stop=True)
             q_bank.append(bank)
 
-        z = [keep.tile([P, D], F32, name="z%d" % t) for t in range(PACK)]
+        z = {}
         u = [keep.tile([P, D], F32, name="u%d" % t) for t in range(PACK)]
         y = keep.tile([P, PACK, D], F32, name="y")
         y_rows = out_0.rearrange("(p t) j -> p t j", t=PACK)
         work = {}
+        s = [keep.tile([P, D], F32, name="s%d" % t) for t in range(2)]
 
         def leave(t, on_vector):
+            z[t] = keep.tile([P, D], F32, name="z%d" % t, tag="window%d" % (t % 2))
             if on_vector:
-                nc.vector.tensor_copy(out=z[t][:], in_=z_bank[t][:])
+                nc.vector.tensor_copy(out=z[t][:], in_=z_bank[t + 1][:])
             else:
-                nc.scalar.copy(out=z[t][:], in_=z_bank[t][:])
+                nc.scalar.copy(out=z[t][:], in_=z_bank[t + 1][:])
 
         def look_up(t, h, on_vector):
             picked = z[t][:].indirect(offsets[:, 16 * h : 16 * (h + 1)])
@@ -111,81 +116,87 @@ def tile_list_head_scaled_by_peak_pl_kernel(tc, xt_words, xt_scales, w, xi_words
                 nc.scalar.activation(out=u[t][:, h * HALF : (h + 1) * HALF], in_=picked, func=ACT.Copy)
 
         def find_peak(t):
-            work[t] = ring.tile([P, 8 + D], F32, name="work")
+            work[t] = ring.tile([P, 8], F32, name="work")
             nc.vector.tensor_reduce(out=work[t][:, 0:1], in_=u[t][:], axis=AXIS.X, op=ALU.max, apply_absolute_value=True)
 
         def add_half(t):
-            nc.vector.tensor_scalar(out=work[t][:, 1:2], in0=work[t][:, 0:1], scalar1=0.5, scalar2=None, op0=ALU.add)
+            nc.vector.tensor_scalar(out=work[t][:, 1:2], in0=work[t][:, 0:1], scalar1=0.5, scalar2=0.3 if t < 2 else 1.0, op0=ALU.add, op1=ALU.mult)
 
         def invert(t):
             nc.vector.reciprocal(out=work[t][:, 2:3], in_=work[t][:, 1:2])
 
         def normalise(t):
-            nc.gpsimd.tensor_scalar(out=work[t][:, 8:], in0=u[t][:], scalar1=work[t][:, 2:3], scalar2=0.0, op0=ALU.mult, op1=ALU.add)
+            nc.gpsimd.tensor_scalar(out=y[:, t, :], in0=s[t][:], scalar1=0.3, scalar2=0.0, op0=ALU.mult, op1=ALU.add)
 
         def scale_q(t):
-            nc.scalar.activation(out=work[t][:, 8:], in_=q_bank[t][:], func=ACT.Copy, scale=0.3)
+            nc.scalar.activation(out=q_part[:, t - 2, :], in_=q_bank[t][:], func=ACT.Copy, scale=0.3)
 
         def combine_from_bank(t):
-            nc.vector.scalar_tensor_tensor(out=y[:, t, :], in0=q_bank[t][:], scalar=0.3, in1=work[t][:, 8:], op0=ALU.mult, op1=ALU.add)
+            nc.vector.scalar_tensor_tensor(out=s[t][:], in0=u[t][:], scalar=work[t][:, 2:3], in1=q_bank[t][:], op0=ALU.mult, op1=ALU.add)
 
         def combine(t, c0, c1):
-            nc.vector.scalar_tensor_tensor(out=y[:, t, c0:c1], in0=u[t][:, c0:c1], scalar=work[t][:, 2:3], in1=work[t][:, 8 + c0 : 8 + c1], op0=ALU.mult, op1=ALU.add)
+            nc.vector.scalar_tensor_tensor(out=y[:, t, c0:c1], in0=u[t][:, c0:c1], scalar=work[t][:, 2:3], in1=q_part[:, t - 2, c0:c1], op0=ALU.mult, op1=ALU.add)
 
         def store(t):
             nc.sync.dma_start(out=y_rows[:, t, :], in_=y[:, t, :])
 
-        leave(0, False)
-        leave(1, True)
+        z[0] = keep.tile([P, D], F32, name="z0", tag="window0")
+        nc.scalar.copy(out=z[0][:, :HALF], in_=z_bank[0][:])
+        nc.vector.tensor_copy(out=z[0][:, HALF:], in_=z_bank[1][:])
         look_up(0, 0, False)
-        look_up(0, 1, False)
-        look_up(1, 0, True)
+        look_up(0, 1, True)
+        leave(1, True)
+        look_up(1, 0, False)
         look_up(1, 1, False)
         find_peak(0)
-        leave(2, False)
-        find_peak(1)
         add_half(0)
-        add_half(1)
+        leave(2, False)
+        leave(3, True)
         invert(0)
-        invert(1)
-        normalise(0)
-        normalise(1)
+        find_peak(1)
+        add_half(1)
         look_up(2, 0, False)
         look_up(2, 1, False)
-        leave(3, True)
         look_up(3, 0, False)
         look_up(3, 1, False)
-        find_peak(2)
+        q_part = keep.tile([P, 2, D], F32, name="q_part", tag="window1")
         scale_q(2)
+        scale_q(3)
         combine_from_bank(0)
+        normalise(0)
         store(0)
+        invert(1)
+        find_peak(2)
         add_half(2)
         combine_from_bank(1)
+        normalise(1)
         store(1)
         invert(2)
         find_peak(3)
-        scale_q(3)
         add_half(3)
-        combine(2, 0, D)
-        store(2)
+        combine(2, 0, HALF)
         invert(3)
-        combine(3, 0, HALF)
-        combine(3, HALF, D)
+        combine(2, HALF, D)
+        store(2)
+        combine(3, 0, WEAVE_SPLIT)
+        combine(3, WEAVE_SPLIT, D)
         store(3)
 
         y_codes = keep.tile([P, D], U32, name="y_codes", align_bytes=64)
         y_plane = keep.tile([P, D], U8, name="y_plane", align_bytes=64)
         y_bf = [keep.tile([P, HALF, PACK], BF16, name="y_bf%d" % h, align_bytes=64) for h in range(2)]
 
-        def weave_views(h):
-            dst = y_bf[h][:].rearrange("p (c i) t -> p c t i", i=4)
-            src = y[:, :, h * HALF : (h + 1) * HALF].rearrange("p t (c i) -> p c t i", i=4)
+        def weave_views(c0, c1):
+            h = c0 // HALF
+            dst = y_bf[h][:, c0 - h * HALF : c1 - h * HALF, :].rearrange("p (c i) t -> p c t i", i=4)
+            src = y[:, :, c0:c1].rearrange("p t (c i) -> p c t i", i=4)
             return dst, src
 
-        dst, src = weave_views(0)
+        dst, src = weave_views(0, WEAVE_SPLIT)
         nc.scalar.activation(out=dst, in_=src, func=ACT.Copy)
-        dst, src = weave_views(1)
-        nc.vector.tensor_copy(out=dst, in_=src)
+        for c0, c1 in ((HALF, D), (WEAVE_SPLIT, HALF)):
+            dst, src = weave_views(c0, c1)
+            nc.vector.tensor_copy(out=dst, in_=src)
         code_rows = out_1[0].rearrange("p c r -> p (c r)").bitcast(I32)
         for h in (1, 0):
             cols = slice(h * HALF, (h + 1) * HALF)

@@ -30,8 +30,8 @@ def tile_list_head_scaled_by_peak_pl_kernel(tc, xt_words, xt_scales, w, xi_words
         ring = ctx.enter_context(tc.tile_pool(name="ring", bufs=2))
         psum = ctx.enter_context(tc.psum_pool(name="psum", bufs=1))
 
-        def load_scales(queue, plane, rows):
-            for quad in range(4):
+        def load_scales(queue, plane, rows, quads=range(4)):
+            for quad in quads:
                 queue.dma_start(out=plane[32 * quad : 32 * quad + 4, :].bitcast(I32), in_=rows[0, 4 * quad : 4 * quad + 4, :].bitcast(I32))
 
         xt_plane = keep.tile([P, D], U8, name="xt_plane", align_bytes=64)
@@ -41,7 +41,7 @@ def tile_list_head_scaled_by_peak_pl_kernel(tc, xt_words, xt_scales, w, xi_words
         nc.gpsimd.memset(wi_plane_raw[:].bitcast(I32), 0)
         nc.vector.memset(xi_plane[:].bitcast(I32), 0)
 
-        load_scales(nc.gpsimd, wi_plane_raw, wi_scales)
+        load_scales(nc.gpsimd, wi_plane_raw, wi_scales, range(1, 4))
         w_rows = w.rearrange("(p j) c -> p j c", j=PACK)
         w_raw = []
         for h, (m0, m1, m2) in enumerate(W_CHUNKS):
@@ -57,6 +57,7 @@ def tile_list_head_scaled_by_peak_pl_kernel(tc, xt_words, xt_scales, w, xi_words
         nc.sync.dma_start(offsets[:], offs)
         xi_codes = keep.tile([P, PACK * D], U8, name="xi_codes", align_bytes=64)
         nc.sync.dma_start(out=xi_codes[:].bitcast(I32), in_=xi_words[0].rearrange("p c r -> p (c r)").bitcast(I32))
+        load_scales(nc.sync, wi_plane_raw, wi_scales, range(1))
         load_scales(nc.sync, xi_plane, xi_scales)
 
         w_bf = keep.tile([P, PACK, P, PACK], BF16, name="w_bf", tag="staging", align_bytes=64)
@@ -99,10 +100,9 @@ def tile_list_head_scaled_by_peak_pl_kernel(tc, xt_words, xt_scales, w, xi_words
         y = keep.tile([P, PACK, D], F32, name="y")
         y_rows = out_0.rearrange("(p t) j -> p t j", t=PACK)
         work = {}
-        s = [keep.tile([P, D], F32, name="s%d" % t) for t in range(2)]
 
         def leave(t, on_vector):
-            z[t] = keep.tile([P, D], F32, name="z%d" % t, tag="window%d" % (t % 2))
+            z[t] = keep.tile([P, D], F32, name="z%d" % t, tag="window%d" % t)
             if on_vector:
                 nc.vector.tensor_copy(out=z[t][:], in_=z_bank[t + 1][:])
             else:
@@ -126,13 +126,13 @@ def tile_list_head_scaled_by_peak_pl_kernel(tc, xt_words, xt_scales, w, xi_words
             nc.vector.reciprocal(out=work[t][:, 2:3], in_=work[t][:, 1:2])
 
         def normalise(t):
-            nc.gpsimd.tensor_scalar(out=y[:, t, :], in0=s[t][:], scalar1=0.3, scalar2=0.0, op0=ALU.mult, op1=ALU.add)
+            nc.gpsimd.tensor_scalar(out=y[:, t, :], in0=y[:, t + 2, :], scalar1=0.3, scalar2=0.0, op0=ALU.mult, op1=ALU.add)
 
         def scale_q(t):
             nc.scalar.activation(out=q_part[:, t - 2, :], in_=q_bank[t][:], func=ACT.Copy, scale=0.3)
 
         def combine_from_bank(t):
-            nc.vector.scalar_tensor_tensor(out=s[t][:], in0=u[t][:], scalar=work[t][:, 2:3], in1=q_bank[t][:], op0=ALU.mult, op1=ALU.add)
+            nc.vector.scalar_tensor_tensor(out=y[:, t + 2, :], in0=u[t][:], scalar=work[t][:, 2:3], in1=q_bank[t][:], op0=ALU.mult, op1=ALU.add)
 
         def combine(t, c0, c1):
             nc.vector.scalar_tensor_tensor(out=y[:, t, c0:c1], in0=u[t][:, c0:c1], scalar=work[t][:, 2:3], in1=q_part[:, t - 2, c0:c1], op0=ALU.mult, op1=ALU.add)
@@ -144,13 +144,13 @@ def tile_list_head_scaled_by_peak_pl_kernel(tc, xt_words, xt_scales, w, xi_words
         nc.scalar.copy(out=z[0][:, :HALF], in_=z_bank[0][:])
         nc.vector.tensor_copy(out=z[0][:, HALF:], in_=z_bank[1][:])
         look_up(0, 0, False)
-        look_up(0, 1, True)
+        look_up(0, 1, False)
         leave(1, True)
+        leave(2, True)
         look_up(1, 0, False)
         look_up(1, 1, False)
         find_peak(0)
         add_half(0)
-        leave(2, False)
         leave(3, True)
         invert(0)
         find_peak(1)
@@ -159,7 +159,7 @@ def tile_list_head_scaled_by_peak_pl_kernel(tc, xt_words, xt_scales, w, xi_words
         look_up(2, 1, False)
         look_up(3, 0, False)
         look_up(3, 1, False)
-        q_part = keep.tile([P, 2, D], F32, name="q_part", tag="window1")
+        q_part = keep.tile([P, 2, D], F32, name="q_part", tag="window3")
         scale_q(2)
         scale_q(3)
         combine_from_bank(0)
@@ -179,7 +179,8 @@ def tile_list_head_scaled_by_peak_pl_kernel(tc, xt_words, xt_scales, w, xi_words
         combine(2, HALF, D)
         store(2)
         combine(3, 0, WEAVE_SPLIT)
-        combine(3, WEAVE_SPLIT, D)
+        combine(3, HALF, D)
+        combine(3, WEAVE_SPLIT, HALF)
         store(3)
 
         y_codes = keep.tile([P, D], U32, name="y_codes", align_bytes=64)

@@ -19,8 +19,8 @@ PACK = 4
 D = 512
 HALF = D // 2
 FLOPS = 2 * 2 * D * D * D
-W_CHUNKS = ((0, 52, 80), (80, 112, 128))
-WEAVE_SPLIT = 192
+W_CHUNKS = ((0, 52, 80), (80, 128))
+WEAVE_SPLIT = 224
 
 
 def tile_list_head_scaled_by_peak_pl_kernel(tc, xt_words, xt_scales, w, xi_words, xi_scales, wi_words, wi_scales, offs, out_0, out_1, out_2):
@@ -35,44 +35,52 @@ def tile_list_head_scaled_by_peak_pl_kernel(tc, xt_words, xt_scales, w, xi_words
                 queue.dma_start(out=plane[32 * quad : 32 * quad + 4, :].bitcast(I32), in_=rows[0, 4 * quad : 4 * quad + 4, :].bitcast(I32))
 
         xt_plane = keep.tile([P, D], U8, name="xt_plane", align_bytes=64)
-        xi_plane = keep.tile([P, D], U8, name="xi_plane", align_bytes=64)
         wi_plane_raw = keep.tile([P, D], U8, name="wi_plane_raw", align_bytes=64)
+        xi_plane = keep.tile([P, D], U8, name="xi_plane", align_bytes=64)
         nc.gpsimd.memset(xt_plane[:].bitcast(I32), 0)
         nc.gpsimd.memset(wi_plane_raw[:].bitcast(I32), 0)
         nc.vector.memset(xi_plane[:].bitcast(I32), 0)
 
+        load_scales(nc.scalar, xt_plane, xt_scales, range(3))
+        load_scales(nc.gpsimd, xt_plane, xt_scales, range(3, 4))
         load_scales(nc.gpsimd, wi_plane_raw, wi_scales, range(1, 4))
         w_rows = w.rearrange("(p j) c -> p j c", j=PACK)
         w_raw = []
-        for h, (m0, m1, m2) in enumerate(W_CHUNKS):
-            raw = keep.tile([P, PACK, PACK * (m2 - m0)], F32, name="w_raw%d" % h)
+        for h, (m0, m2) in enumerate(((0, 80), (80, 128))):
+            raw = keep.tile([P, PACK, PACK * (m2 - m0)], F32, name="w_raw%d" % h, align_bytes=64)
             nc.sync.dma_start(out=raw[:], in_=w_rows[:, :, PACK * m0 : PACK * m2])
             w_raw.append(raw)
         xt_codes = keep.tile([P, 2 * D], U8, name="xt_codes", align_bytes=64)
         nc.sync.dma_start(out=xt_codes[:].bitcast(I32), in_=xt_words[0].bitcast(I32))
-        load_scales(nc.sync, xt_plane, xt_scales)
         wi_raw = keep.tile([P, 2 * D], U8, name="wi_raw", align_bytes=64)
         nc.sync.dma_start(out=wi_raw[:].bitcast(I32), in_=wi_words[0].bitcast(I32))
         offsets = keep.tile([P, D // 16], U16, name="offsets")
         nc.sync.dma_start(offsets[:], offs)
-        xi_codes = keep.tile([P, PACK * D], U8, name="xi_codes", align_bytes=64)
-        nc.sync.dma_start(out=xi_codes[:].bitcast(I32), in_=xi_words[0].rearrange("p c r -> p (c r)").bitcast(I32))
         load_scales(nc.sync, wi_plane_raw, wi_scales, range(1))
-        load_scales(nc.sync, xi_plane, xi_scales)
 
         w_bf = keep.tile([P, PACK, P, PACK], BF16, name="w_bf", tag="staging", align_bytes=64)
 
-        def cast_views(h, m0, m1):
+        def cast_views(h, m0, m1, t0, t1):
             first = W_CHUNKS[h][0]
-            dst = w_bf[:, :, m0:m1, :].rearrange("p t m j -> p m t j")
-            src = w_raw[h][:, :, PACK * (m0 - first) : PACK * (m1 - first)].rearrange("p j (m t) -> p m t j", t=PACK)
+            dst = w_bf[:, t0:t1, m0:m1, :].rearrange("p t m j -> p m t j")
+            src = w_raw[h][:, :, PACK * (m0 - first) : PACK * (m1 - first)].rearrange("p j (m t) -> p m t j", t=PACK)[:, :, t0:t1, :]
             return dst, src
 
-        for h, (m0, m1, m2) in enumerate(W_CHUNKS):
-            dst, src = cast_views(h, m0, m1)
+        m0, m1, m2 = W_CHUNKS[0]
+        dst, src = cast_views(0, m0, m1, 0, PACK)
+        nc.vector.tensor_copy(out=dst, in_=src)
+        dst, src = cast_views(0, m1, m2, 0, PACK)
+        nc.scalar.activation(out=dst, in_=src, func=ACT.Copy)
+        m0, m2 = W_CHUNKS[1]
+        for t in range(2):
+            dst, src = cast_views(1, m0, m2, t, t + 1)
             nc.vector.tensor_copy(out=dst, in_=src)
-            dst, src = cast_views(h, m1, m2)
-            nc.scalar.activation(out=dst, in_=src, func=ACT.Copy)
+        dst, src = cast_views(1, m0, m2, 2, PACK)
+        nc.scalar.activation(out=dst, in_=src, func=ACT.Copy)
+
+        xi_codes = keep.tile([P, PACK * D], U8, name="xi_codes", tag="w_raw0", align_bytes=64)
+        nc.sync.dma_start(out=xi_codes[:].bitcast(I32), in_=xi_words[0].rearrange("p c r -> p (c r)").bitcast(I32))
+        load_scales(nc.sync, xi_plane, xi_scales)
 
         z_bank = []
         for t in range(PACK):
@@ -102,7 +110,7 @@ def tile_list_head_scaled_by_peak_pl_kernel(tc, xt_words, xt_scales, w, xi_words
         work = {}
 
         def leave(t, on_vector):
-            z[t] = keep.tile([P, D], F32, name="z%d" % t, tag="window%d" % t)
+            z[t] = keep.tile([P, D], F32, name="z%d" % t, tag="window%d" % (1 if t == 3 else t))
             if on_vector:
                 nc.vector.tensor_copy(out=z[t][:], in_=z_bank[t + 1][:])
             else:
@@ -144,36 +152,38 @@ def tile_list_head_scaled_by_peak_pl_kernel(tc, xt_words, xt_scales, w, xi_words
         nc.scalar.copy(out=z[0][:, :HALF], in_=z_bank[0][:])
         nc.vector.tensor_copy(out=z[0][:, HALF:], in_=z_bank[1][:])
         look_up(0, 0, False)
-        look_up(0, 1, False)
         leave(1, True)
+        look_up(0, 1, True)
         leave(2, True)
         look_up(1, 0, False)
         look_up(1, 1, False)
         find_peak(0)
-        add_half(0)
-        leave(3, True)
-        invert(0)
         find_peak(1)
+        add_half(0)
         add_half(1)
+        invert(0)
+        invert(1)
         look_up(2, 0, False)
         look_up(2, 1, False)
+        leave(3, False)
         look_up(3, 0, False)
         look_up(3, 1, False)
-        q_part = keep.tile([P, 2, D], F32, name="q_part", tag="window3")
+        q_part = keep.tile([P, 2, D], F32, name="q_part", tag="window1")
         scale_q(2)
         scale_q(3)
         combine_from_bank(0)
         normalise(0)
         store(0)
-        invert(1)
         find_peak(2)
         add_half(2)
         combine_from_bank(1)
         normalise(1)
         store(1)
         invert(2)
-        find_peak(3)
-        add_half(3)
+        work[3] = ring.tile([P, 8], F32, name="work")
+        for h in range(2):
+            nc.vector.tensor_reduce(out=work[3][:, 3 + h : 4 + h], in_=u[3][:, h * HALF : (h + 1) * HALF], axis=AXIS.X, op=ALU.max, apply_absolute_value=True)
+        nc.vector.tensor_scalar(out=work[3][:, 1:2], in0=work[3][:, 3:4], scalar1=work[3][:, 4:5], scalar2=0.5, op0=ALU.max, op1=ALU.add)
         combine(2, 0, HALF)
         invert(3)
         combine(2, HALF, D)

from contextlib import ExitStack

import concourse.mybir as mybir

F32 = mybir.dt.float32
BF16 = mybir.dt.bfloat16
I32 = mybir.dt.int32
U32 = mybir.dt.uint32
U16 = mybir.dt.uint16
U8 = mybir.dt.uint8
FP8X4 = mybir.dt.float8_e4m3fn_x4
FP4X4 = mybir.dt.float4_e2m1fn_x4
ALU = mybir.AluOpType
ACT = mybir.ActivationFunctionType
AXIS = mybir.AxisListType

P = 128
PACK = 4
D = 512
HALF = D // 2
FLOPS = 2 * 2 * D * D * D
W_CHUNKS = ((0, 52, 80), (80, 128))
WEAVE_SPLIT = 224


def tile_list_head_scaled_by_peak_pl_kernel(tc, xt_words, xt_scales, w, xi_words, xi_scales, wi_words, wi_scales, offs, out_0, out_1, out_2):
    nc = tc.nc
    with ExitStack() as ctx:
        keep = ctx.enter_context(tc.tile_pool(name="keep", bufs=1))
        ring = ctx.enter_context(tc.tile_pool(name="ring", bufs=2))
        psum = ctx.enter_context(tc.psum_pool(name="psum", bufs=1))

        def load_scales(queue, plane, rows, quads=range(4)):
            for quad in quads:
                queue.dma_start(out=plane[32 * quad : 32 * quad + 4, :].bitcast(I32), in_=rows[0, 4 * quad : 4 * quad + 4, :].bitcast(I32))

        xt_plane = keep.tile([P, D], U8, name="xt_plane", align_bytes=64)
        wi_plane_raw = keep.tile([P, D], U8, name="wi_plane_raw", align_bytes=64)
        xi_plane = keep.tile([P, D], U8, name="xi_plane", align_bytes=64)
        nc.gpsimd.memset(xt_plane[:].bitcast(I32), 0)
        nc.gpsimd.memset(wi_plane_raw[:].bitcast(I32), 0)
        nc.vector.memset(xi_plane[:].bitcast(I32), 0)

        load_scales(nc.scalar, xt_plane, xt_scales, range(3))
        load_scales(nc.gpsimd, xt_plane, xt_scales, range(3, 4))
        load_scales(nc.gpsimd, wi_plane_raw, wi_scales, range(1, 4))
        w_rows = w.rearrange("(p j) c -> p j c", j=PACK)
        w_raw = []
        for h, (m0, m2) in enumerate(((0, 80), (80, 128))):
            raw = keep.tile([P, PACK, PACK * (m2 - m0)], F32, name="w_raw%d" % h, align_bytes=64)
            nc.sync.dma_start(out=raw[:], in_=w_rows[:, :, PACK * m0 : PACK * m2])
            w_raw.append(raw)
        xt_codes = keep.tile([P, 2 * D], U8, name="xt_codes", align_bytes=64)
        nc.sync.dma_start(out=xt_codes[:].bitcast(I32), in_=xt_words[0].bitcast(I32))
        wi_raw = keep.tile([P, 2 * D], U8, name="wi_raw", align_bytes=64)
        nc.sync.dma_start(out=wi_raw[:].bitcast(I32), in_=wi_words[0].bitcast(I32))
        offsets = keep.tile([P, D // 16], U16, name="offsets")
        nc.sync.dma_start(offsets[:], offs)
        load_scales(nc.sync, wi_plane_raw, wi_scales, range(1))

        w_bf = keep.tile([P, PACK, P, PACK], BF16, name="w_bf", tag="staging", align_bytes=64)

        def cast_views(h, m0, m1, t0, t1):
            first = W_CHUNKS[h][0]
            dst = w_bf[:, t0:t1, m0:m1, :].rearrange("p t m j -> p m t j")
            src = w_raw[h][:, :, PACK * (m0 - first) : PACK * (m1 - first)].rearrange("p j (m t) -> p m t j", t=PACK)[:, :, t0:t1, :]
            return dst, src

        m0, m1, m2 = W_CHUNKS[0]
        dst, src = cast_views(0, m0, m1, 0, PACK)
        nc.vector.tensor_copy(out=dst, in_=src)
        dst, src = cast_views(0, m1, m2, 0, PACK)
        nc.scalar.activation(out=dst, in_=src, func=ACT.Copy)
        m0, m2 = W_CHUNKS[1]
        for t in range(2):
            dst, src = cast_views(1, m0, m2, t, t + 1)
            nc.vector.tensor_copy(out=dst, in_=src)
        dst, src = cast_views(1, m0, m2, 2, PACK)
        nc.scalar.activation(out=dst, in_=src, func=ACT.Copy)

        xi_codes = keep.tile([P, PACK * D], U8, name="xi_codes", tag="w_raw0", align_bytes=64)
        nc.sync.dma_start(out=xi_codes[:].bitcast(I32), in_=xi_words[0].rearrange("p c r -> p (c r)").bitcast(I32))
        load_scales(nc.sync, xi_plane, xi_scales)

        z_bank = []
        for t in range(PACK):
            codes = keep.tile([P, P], U32, name="w_codes%d" % t, align_bytes=64)
            plane = keep.tile([P, P], U8, name="w_plane%d" % t, align_bytes=64)
            nc.vector.quantize_mx(out=codes[:].bitcast(FP8X4), scales=plane[:], in_=w_bf[:, t, :, :].rearrange("p m j -> p (m j)"))
            width = HALF if t == 0 else D
            for c0 in range(0, D, width):
                bank = psum.tile([P, width], F32, name="z_bank%d" % len(z_bank))
                nc.tensor.matmul_mx(out=bank[:], lhsT=codes[:].bitcast(FP8X4), lhsT_scale=plane[:], rhs=xt_codes[:, 2 * c0 : 2 * (c0 + width)].bitcast(FP4X4), rhs_scale=xt_plane[:, c0 : c0 + width], start=True, stop=True)
                z_bank.append(bank)

        wi_codes = keep.tile([P, 2 * D], U8, name="wi_codes", align_bytes=64)
        wi_plane = keep.tile([P, D], U8, name="wi_plane", tag="staging", align_bytes=64)
        nc.scalar.copy(out=wi_codes[:].bitcast(U16).rearrange("p (t m) -> p t m", t=PACK), in_=wi_raw[:].bitcast(U16).rearrange("p (m t) -> p t m", t=PACK))
        nc.gpsimd.tensor_copy(out=wi_plane[:].rearrange("p (t m) -> p t m", t=PACK), in_=wi_plane_raw[:].rearrange("p (m t) -> p t m", t=PACK))
        q_bank = []
        for t in range(PACK):
            bank = psum.tile([P, D], F32, name="q_bank%d" % t, tag="z_bank0" if t == 3 else "q_bank%d" % t)
            nc.tensor.matmul_mx(out=bank[:], lhsT=wi_codes[:, 2 * P * t : 2 * P * (t + 1)].bitcast(FP4X4), lhsT_scale=wi_plane[:, P * t : P * (t + 1)], rhs=xi_codes[:].bitcast(FP8X4), rhs_scale=xi_plane[:], start=True, stop=True)
            q_bank.append(bank)

        z = {}
        u = [keep.tile([P, D], F32, name="u%d" % t) for t in range(PACK)]
        y = keep.tile([P, PACK, D], F32, name="y")
        y_rows = out_0.rearrange("(p t) j -> p t j", t=PACK)
        work = {}

        def leave(t, on_vector):
            z[t] = keep.tile([P, D], F32, name="z%d" % t, tag="window%d" % (1 if t == 3 else t))
            if on_vector:
                nc.vector.tensor_copy(out=z[t][:], in_=z_bank[t + 1][:])
            else:
                nc.scalar.copy(out=z[t][:], in_=z_bank[t + 1][:])

        def look_up(t, h, on_vector):
            picked = z[t][:].indirect(offsets[:, 16 * h : 16 * (h + 1)])
            if on_vector:
                nc.vector.tensor_copy(out=u[t][:, h * HALF : (h + 1) * HALF], in_=picked)
            else:
                nc.scalar.activation(out=u[t][:, h * HALF : (h + 1) * HALF], in_=picked, func=ACT.Copy)

        def find_peak(t):
            work[t] = ring.tile([P, 8], F32, name="work")
            nc.vector.tensor_reduce(out=work[t][:, 0:1], in_=u[t][:], axis=AXIS.X, op=ALU.max, apply_absolute_value=True)

        def add_half(t):
            nc.vector.tensor_scalar(out=work[t][:, 1:2], in0=work[t][:, 0:1], scalar1=0.5, scalar2=0.3 if t < 2 else 1.0, op0=ALU.add, op1=ALU.mult)

        def invert(t):
            nc.vector.reciprocal(out=work[t][:, 2:3], in_=work[t][:, 1:2])

        def normalise(t):
            nc.gpsimd.tensor_scalar(out=y[:, t, :], in0=y[:, t + 2, :], scalar1=0.3, scalar2=0.0, op0=ALU.mult, op1=ALU.add)

        def scale_q(t):
            nc.scalar.activation(out=q_part[:, t - 2, :], in_=q_bank[t][:], func=ACT.Copy, scale=0.3)

        def combine_from_bank(t):
            nc.vector.scalar_tensor_tensor(out=y[:, t + 2, :], in0=u[t][:], scalar=work[t][:, 2:3], in1=q_bank[t][:], op0=ALU.mult, op1=ALU.add)

        def combine(t, c0, c1):
            nc.vector.scalar_tensor_tensor(out=y[:, t, c0:c1], in0=u[t][:, c0:c1], scalar=work[t][:, 2:3], in1=q_part[:, t - 2, c0:c1], op0=ALU.mult, op1=ALU.add)

        def store(t):
            nc.sync.dma_start(out=y_rows[:, t, :], in_=y[:, t, :])

        z[0] = keep.tile([P, D], F32, name="z0", tag="window0")
        nc.scalar.copy(out=z[0][:, :HALF], in_=z_bank[0][:])
        nc.vector.tensor_copy(out=z[0][:, HALF:], in_=z_bank[1][:])
        look_up(0, 0, False)
        leave(1, True)
        look_up(0, 1, True)
        leave(2, True)
        look_up(1, 0, False)
        look_up(1, 1, False)
        find_peak(0)
        find_peak(1)
        add_half(0)
        add_half(1)
        invert(0)
        invert(1)
        look_up(2, 0, False)
        look_up(2, 1, False)
        leave(3, False)
        look_up(3, 0, False)
        look_up(3, 1, False)
        q_part = keep.tile([P, 2, D], F32, name="q_part", tag="window1")
        scale_q(2)
        scale_q(3)
        combine_from_bank(0)
        normalise(0)
        store(0)
        find_peak(2)
        add_half(2)
        combine_from_bank(1)
        normalise(1)
        store(1)
        invert(2)
        work[3] = ring.tile([P, 8], F32, name="work")
        for h in range(2):
            nc.vector.tensor_reduce(out=work[3][:, 3 + h : 4 + h], in_=u[3][:, h * HALF : (h + 1) * HALF], axis=AXIS.X, op=ALU.max, apply_absolute_value=True)
        nc.vector.tensor_scalar(out=work[3][:, 1:2], in0=work[3][:, 3:4], scalar1=work[3][:, 4:5], scalar2=0.5, op0=ALU.max, op1=ALU.add)
        combine(2, 0, HALF)
        invert(3)
        combine(2, HALF, D)
        store(2)
        combine(3, 0, WEAVE_SPLIT)
        combine(3, HALF, D)
        combine(3, WEAVE_SPLIT, HALF)
        store(3)

        y_codes = keep.tile([P, D], U32, name="y_codes", align_bytes=64)
        y_plane = keep.tile([P, D], U8, name="y_plane", align_bytes=64)
        y_bf = [keep.tile([P, HALF, PACK], BF16, name="y_bf%d" % h, align_bytes=64) for h in range(2)]

        def weave_views(c0, c1):
            h = c0 // HALF
            dst = y_bf[h][:, c0 - h * HALF : c1 - h * HALF, :].rearrange("p (c i) t -> p c t i", i=4)
            src = y[:, :, c0:c1].rearrange("p t (c i) -> p c t i", i=4)
            return dst, src

        dst, src = weave_views(0, WEAVE_SPLIT)
        nc.scalar.activation(out=dst, in_=src, func=ACT.Copy)
        for c0, c1 in ((HALF, D), (WEAVE_SPLIT, HALF)):
            dst, src = weave_views(c0, c1)
            nc.vector.tensor_copy(out=dst, in_=src)
        code_rows = out_1[0].rearrange("p c r -> p (c r)").bitcast(I32)
        for h in (1, 0):
            cols = slice(h * HALF, (h + 1) * HALF)
            nc.vector.quantize_mx(out=y_codes[:, cols].bitcast(FP8X4), scales=y_plane[:, cols], in_=y_bf[h][:].rearrange("p c t -> p (c t)"))
            nc.sync.dma_start(out=code_rows[:, cols], in_=y_codes[:, cols].bitcast(I32))
        for quad in range(4):
            queue = nc.sync if quad == 3 else nc.scalar
            queue.dma_start(out=out_2[0, 4 * quad : 4 * quad + 4, :].bitcast(I32), in_=y_plane[32 * quad : 32 * quad + 4, :].bitcast(I32))
